import numpy as np
import ml_dtypes


def mxq(x, axis, fmt="e4m3"):
    dtype, down = {"e4m3": (ml_dtypes.float8_e4m3fn, 7), "e5m2": (ml_dtypes.float8_e5m2, 14)}[fmt]
    v = np.moveaxis(np.asarray(x, np.float32).astype(ml_dtypes.bfloat16).astype(np.float64), axis, -1)
    blocks = v.reshape(v.shape[:-1] + (-1, 32))
    amax = np.abs(blocks).max(-1, keepdims=True)
    byte = np.maximum(np.where(amax > 0, np.frexp(amax)[1] - 1 + 127, 0) - down, 1)
    scale = np.exp2(byte - 127.0)
    codes = (blocks / scale).astype(np.float32).astype(dtype).astype(np.float64)
    return np.moveaxis((codes * scale).reshape(v.shape), -1, axis)


WIDE = False


def mx_kscale(k):
    if not WIDE:
        return np.ones(k)
    levels = np.array([10, -10, 5, -5, 0])
    if k % 512:
        return np.exp2(np.random.permutation(np.resize(levels, k // 32))).repeat(32)
    a = np.empty((k // 512, 16))
    for p in range(k // 512):
        a[p, :8] = np.random.permutation(np.resize(levels, 8))
        for g in range(8):
            far = levels[np.abs(levels - a[p, g]) >= 10]
            a[p, g + 8] = far[np.random.randint(len(far))]
    return np.exp2(a.ravel()).repeat(32)


def f64(x):
    return np.asarray(x).astype(np.float64)


def striped(idx):
    return np.tile(idx.reshape(-1, 16).T, (8, 1)).astype(np.uint16)


def unstriped(offs):
    return offs[:16].T.reshape(-1).astype(np.int64)


def pack_weight(w):
    k, n = w.shape
    w = f64(np.asarray(w, np.float32).astype(ml_dtypes.bfloat16)).reshape(k // 32, 32, n)
    amax = np.abs(w).max(1)
    byte = np.clip(np.where(amax > 0, np.frexp(amax)[1] - 1 + 127 - 7, 1), 1, 254)
    scaled = (w * np.exp2(127.0 - byte)[:, None, :]).reshape(k, n).astype(np.float32)
    words = np.ascontiguousarray(scaled.reshape(k // 512, 128, 4, n).transpose(0, 1, 3, 2)).astype(ml_dtypes.float8_e4m3fn).view(np.uint8)
    return words, np.ascontiguousarray(byte.astype(np.uint8).reshape(k // 512, 16, n))


def unpack_weight(words, scales):
    g, p, n, _ = words.shape
    vals = np.ascontiguousarray(words).view(ml_dtypes.float8_e4m3fn).astype(np.float64) * np.repeat(np.exp2(scales.astype(np.float64) - 127.0), 8, axis=1)[..., None]
    return vals.transpose(0, 1, 3, 2).reshape(g * 512, n)


def relu(v):
    return np.maximum(v, 0.0)


K, T, S, N = 512, 2048, 768, 256


def setup_inputs():
    n = np.random.standard_normal
    s = mx_kscale(K)[:, None]
    w1, w2 = n((2, K, N)) / np.sqrt(2 * K) / s[None]
    p1, p2 = pack_weight(w1), pack_weight(w2)
    return {
        "xT": (n((K, S)) * s).astype(np.float32),
        "sT": (n((K, T)) * s).astype(np.float32),
        "w1_words": p1[0],
        "w1_scales": p1[1],
        "w2_words": p2[0],
        "w2_scales": p2[1],
        "b": (0.3 * n((N, 1))).astype(np.float32),
        "offs": striped(np.random.permutation(T)[:S]),
    }


def reference(xT, sT, w1_words, w1_scales, w2_words, w2_scales, b, offs):
    y = unpack_weight(w1_words, w1_scales).T @ mxq(f64(xT), 0, "e4m3") + unpack_weight(w2_words, w2_scales).T @ mxq(f64(sT)[:, unstriped(offs)], 0, "e4m3")
    return relu(y + f64(b))

@@ -1,0 +1,160 @@
+from contextlib import ExitStack
+
+import concourse.mybir as mybir
+
+K, T, S, N = 512, 2048, 768, 256
+FLOPS = 2 * 2 * K * N * S
+
+F32 = mybir.dt.float32
+BF16 = mybir.dt.bfloat16
+I32 = mybir.dt.int32
+U32 = mybir.dt.uint32
+U16 = mybir.dt.uint16
+U8 = mybir.dt.uint8
+FP8X4 = mybir.dt.float8_e4m3fn_x4
+ACT = mybir.ActivationFunctionType
+ALU = mybir.AluOpType
+
+P = 128
+PACK = 4
+CHUNK = 256
+CHUNKS = S // CHUNK
+HALVES = N // P
+SCALE_WORDS = N // 4
+
+
+def tile_picked_recall_relu_e_kernel(tc, xT, sT, w1_words, w1_scales, w2_words, w2_scales, b, offs, out):
+    nc = tc.nc
+    with ExitStack() as ctx:
+        keep = ctx.enter_context(tc.tile_pool(name="keep", bufs=1))
+        psum = ctx.enter_context(tc.psum_pool(name="psum", bufs=1))
+
+        offsets = keep.tile([P, S // 16], U16, name="offsets")
+        s_plane = [keep.tile([P, T], F32, name=f"s_plane{t}") for t in range(PACK)]
+        x_raw = [keep.tile([P, PACK, CHUNK], F32, name=f"x_raw{c}") for c in range(CHUNKS)]
+        w_codes = [keep.tile([P, N], I32, name=f"w_codes{i}", align_bytes=64) for i in range(2)]
+        w_scale = keep.tile([P, 2, SCALE_WORDS], I32, name="w_scale", align_bytes=64)
+        bias = [keep.tile([P, 1], F32, name=f"bias{h}") for h in range(HALVES)]
+        warm = keep.tile([P, 2], F32, name="warm")
+        s_low = keep.tile([P, 2, S], F32, name="s_low")
+        s_grouped = keep.tile([P, S, PACK], BF16, name="s_grouped", align_bytes=64)
+        x_grouped = keep.tile([P, S, PACK], BF16, name="x_grouped", align_bytes=64)
+        s_codes = keep.tile([P, S], U32, name="s_codes", align_bytes=64)
+        x_codes = keep.tile([P, S], U32, name="x_codes", align_bytes=64)
+        s_scale = keep.tile([P, S], U8, name="s_scale", align_bytes=64)
+        x_scale = keep.tile([P, S], U8, name="x_scale", align_bytes=64)
+        result = [keep.tile([P, HALVES, CHUNK], F32, name=f"result{c}") for c in range(CHUNKS)]
+        acc = [[psum.tile([P, CHUNK], F32, name=f"acc{c}_{h}") for h in range(HALVES)] for c in range(CHUNKS)]
+
+        s_rows = sT.rearrange("(p t) j -> t p j", t=PACK)
+        x_rows = xT.rearrange("(p t) j -> p t j", t=PACK)
+        out_rows = out.rearrange("(h p) j -> p h j", p=P)
+
+        def cols(c):
+            return slice(c * CHUNK, (c + 1) * CHUNK)
+
+        def load_plane(t):
+            nc.sync.dma_start(out=s_plane[t][:], in_=s_rows[t])
+
+        def load_x(c):
+            nc.sync.dma_start(out=x_raw[c][:], in_=x_rows[:, :, cols(c)])
+
+        def load_codes(i, words):
+            nc.sync.dma_start(out=w_codes[i][:], in_=words[0].rearrange("p m r -> p (m r)").bitcast(I32))
+
+        def load_scales(i, scales):
+            rows = scales[0].bitcast(I32)
+            for q in range(4):
+                nc.gpsimd.dma_start(out=w_scale[32 * q : 32 * q + 4, i, :], in_=rows[4 * q : 4 * q + 4, :])
+
+        def picked(t, c):
+            return s_plane[t][:].indirect(offsets[:, c * (CHUNK // 16) : (c + 1) * (CHUNK // 16)])
+
+        def group_x(copy, c, a, z):
+            src = x_raw[c][:, :, a:z].rearrange("p t (g i) -> p g t i", i=4)
+            dst = x_grouped[:, c * CHUNK + a : c * CHUNK + z, :].rearrange("p (g i) t -> p g t i", i=4)
+            copy(dst, src)
+
+        def scalar_copy(dst, src):
+            nc.scalar.activation(dst, src, ACT.Copy)
+
+        def quantize(grouped, codes, scale, c):
+            nc.vector.quantize_mx(
+                out=codes[:, cols(c)].bitcast(FP8X4),
+                scales=scale[:, cols(c)],
+                in_=grouped[:, cols(c), :].rearrange("p j t -> p (j t)"),
+            )
+
+        def multiply(i, codes, scale, c, first):
+            for h in range(HALVES):
+                nc.tensor.matmul_mx(
+                    out=acc[c][h][:],
+                    lhsT=w_codes[i][:, h * P : (h + 1) * P].bitcast(FP8X4),
+                    lhsT_scale=w_scale[:, i, h * P // 4 : (h + 1) * P // 4].bitcast(U8),
+                    rhs=codes[:, cols(c)].bitcast(FP8X4),
+                    rhs_scale=scale[:, cols(c)],
+                    start=first,
+                    stop=not first,
+                )
+
+        def relu_scalar(c, h):
+            nc.scalar.activation(result[c][:, h, :], acc[c][h][:], ACT.Relu, bias=bias[h][:])
+
+        def relu_vector(c, h):
+            nc.vector.tensor_scalar(result[c][:, h, :], acc[c][h][:], bias[h][:], 0.0, ALU.add, ALU.max)
+
+        def store(c):
+            nc.sync.dma_start(out=out_rows[:, :, cols(c)], in_=result[c][:])
+
+        nc.gpsimd.memset(w_scale[:], 0)
+        nc.vector.memset(warm[:, 0:1], 0.0)
+        nc.scalar.activation(warm[:, 1:2], warm[:, 0:1], ACT.Relu)
+
+        load_plane(2)
+        nc.sync.dma_start(offsets[:], offs)
+        load_scales(1, w2_scales)
+        load_plane(0)
+        load_plane(1)
+        load_scales(0, w1_scales)
+        load_plane(3)
+        for h in range(HALVES):
+            nc.scalar.dma_start(out=bias[h][:], in_=b[h * P : (h + 1) * P, :])
+        load_x(0)
+        load_codes(1, w2_words)
+        load_x(1)
+        load_codes(0, w1_words)
+        load_x(2)
+
+        nc.vector.tensor_copy(s_grouped[:, :, 2], s_plane[2][:].indirect(offsets[:]))
+        nc.vector.tensor_copy(s_low[:, 0, :], s_plane[0][:].indirect(offsets[:]))
+        for c in range(CHUNKS):
+            nc.vector.tensor_copy(s_low[:, 1, cols(c)], picked(1, c))
+            scalar_copy(s_grouped[:, cols(c), 0:2], s_low[:, :, cols(c)].rearrange("p t j -> p j t"))
+
+        nc.vector.tensor_copy(s_grouped[:, cols(0), 3], picked(3, 0))
+        nc.vector.tensor_copy(s_grouped[:, cols(1), 3], picked(3, 1))
+        quantize(s_grouped, s_codes, s_scale, 0)
+        group_x(scalar_copy, 0, 0, CHUNK)
+        nc.vector.tensor_copy(s_grouped[:, cols(2), 3], picked(3, 2))
+        quantize(s_grouped, s_codes, s_scale, 1)
+        multiply(1, s_codes, s_scale, 0, True)
+        multiply(1, s_codes, s_scale, 1, True)
+        quantize(x_grouped, x_codes, x_scale, 0)
+        quantize(s_grouped, s_codes, s_scale, 2)
+        group_x(scalar_copy, 1, 0, CHUNK)
+        multiply(1, s_codes, s_scale, 2, True)
+        multiply(0, x_codes, x_scale, 0, False)
+        quantize(x_grouped, x_codes, x_scale, 1)
+        multiply(0, x_codes, x_scale, 1, False)
+        group_x(nc.vector.tensor_copy, 2, 0, CHUNK)
+        for h in range(HALVES):
+            relu_scalar(0, h)
+        store(0)
+        quantize(x_grouped, x_codes, x_scale, 2)
+        multiply(0, x_codes, x_scale, 2, False)
+        for h in range(HALVES):
+            relu_scalar(1, h)
+        store(1)
+        relu_vector(2, 0)
+        relu_scalar(2, 1)
+        store(2)

@@ -23,6 +23,9 @@ HALVES = N // P
 SCALE_WORDS = N // 4
 
 
+X_PIECES = ((0, 256), (256, 512), (512, 640), (640, 768))
+
+
 def tile_picked_recall_relu_e_kernel(tc, xT, sT, w1_words, w1_scales, w2_words, w2_scales, b, offs, out):
     nc = tc.nc
     with ExitStack() as ctx:
@@ -31,8 +34,8 @@ def tile_picked_recall_relu_e_kernel(tc, xT, sT, w1_words, w1_scales, w2_words, 
 
         offsets = keep.tile([P, S // 16], U16, name="offsets")
         s_plane = [keep.tile([P, T], F32, name=f"s_plane{t}") for t in range(PACK)]
-        x_raw = [keep.tile([P, PACK, CHUNK], F32, name=f"x_raw{c}") for c in range(CHUNKS)]
-        w_codes = [keep.tile([P, N], I32, name=f"w_codes{i}", align_bytes=64) for i in range(2)]
+        x_raw = keep.tile([P, PACK * S], F32, name="x_raw")
+        w_codes = keep.tile([P, 2, N], I32, name="w_codes", align_bytes=64)
         w_scale = keep.tile([P, 2, SCALE_WORDS], I32, name="w_scale", align_bytes=64)
         bias = [keep.tile([P, 1], F32, name=f"bias{h}") for h in range(HALVES)]
         warm = keep.tile([P, 2], F32, name="warm")
@@ -43,8 +46,8 @@ def tile_picked_recall_relu_e_kernel(tc, xT, sT, w1_words, w1_scales, w2_words, 
         x_codes = keep.tile([P, S], U32, name="x_codes", align_bytes=64)
         s_scale = keep.tile([P, S], U8, name="s_scale", align_bytes=64)
         x_scale = keep.tile([P, S], U8, name="x_scale", align_bytes=64)
-        result = [keep.tile([P, HALVES, CHUNK], F32, name=f"result{c}") for c in range(CHUNKS)]
-        acc = [[psum.tile([P, CHUNK], F32, name=f"acc{c}_{h}") for h in range(HALVES)] for c in range(CHUNKS)]
+        result = [keep.tile([P, HALVES, z - a], F32, name=f"result{i}") for i, (a, z) in enumerate(X_PIECES)]
+        acc = [[psum.tile([P, z - a], F32, name=f"acc{i}_{h}") for h in range(HALVES)] for i, (a, z) in enumerate(X_PIECES)]
 
         s_rows = sT.rearrange("(p t) j -> t p j", t=PACK)
         x_rows = xT.rearrange("(p t) j -> p t j", t=PACK)
@@ -53,77 +56,89 @@ def tile_picked_recall_relu_e_kernel(tc, xT, sT, w1_words, w1_scales, w2_words, 
         def cols(c):
             return slice(c * CHUNK, (c + 1) * CHUNK)
 
+        def piece(i):
+            return slice(*X_PIECES[i])
+
+        def x_piece(i):
+            a, z = X_PIECES[i]
+            return x_raw[:, PACK * a : PACK * z].rearrange("p (t j) -> p t j", t=PACK)
+
         def load_plane(t):
             nc.sync.dma_start(out=s_plane[t][:], in_=s_rows[t])
 
-        def load_x(c):
-            nc.sync.dma_start(out=x_raw[c][:], in_=x_rows[:, :, cols(c)])
+        def load_x(i):
+            nc.sync.dma_start(out=x_piece(i), in_=x_rows[:, :, piece(i)])
 
-        def load_codes(i, words):
-            nc.sync.dma_start(out=w_codes[i][:], in_=words[0].rearrange("p m r -> p (m r)").bitcast(I32))
+        def load_codes(w, words):
+            nc.sync.dma_start(out=w_codes[:, w, :], in_=words[0].rearrange("p m r -> p (m r)").bitcast(I32))
 
-        def load_scales(i, scales):
+        def load_scales(w, scales):
             rows = scales[0].bitcast(I32)
             for q in range(4):
-                nc.gpsimd.dma_start(out=w_scale[32 * q : 32 * q + 4, i, :], in_=rows[4 * q : 4 * q + 4, :])
+                nc.sync.dma_start(out=w_scale[32 * q : 32 * q + 4, w, :], in_=rows[4 * q : 4 * q + 4, :])
 
         def picked(t, c):
             return s_plane[t][:].indirect(offsets[:, c * (CHUNK // 16) : (c + 1) * (CHUNK // 16)])
 
-        def group_x(copy, c, a, z):
-            src = x_raw[c][:, :, a:z].rearrange("p t (g i) -> p g t i", i=4)
-            dst = x_grouped[:, c * CHUNK + a : c * CHUNK + z, :].rearrange("p (g i) t -> p g t i", i=4)
+        def group_x(copy, i):
+            src = x_piece(i).rearrange("p t (g e) -> p g t e", e=4)
+            dst = x_grouped[:, piece(i), :].rearrange("p (g e) t -> p g t e", e=4)
             copy(dst, src)
 
         def scalar_copy(dst, src):
             nc.scalar.activation(dst, src, ACT.Copy)
 
-        def quantize(grouped, codes, scale, c):
+        def quantize(grouped, codes, scale, js):
             nc.vector.quantize_mx(
-                out=codes[:, cols(c)].bitcast(FP8X4),
-                scales=scale[:, cols(c)],
-                in_=grouped[:, cols(c), :].rearrange("p j t -> p (j t)"),
+                out=codes[:, js].bitcast(FP8X4),
+                scales=scale[:, js],
+                in_=grouped[:, js, :].rearrange("p j t -> p (j t)"),
             )
 
-        def multiply(i, codes, scale, c, first):
+        def multiply(w, codes, scale, i, first):
             for h in range(HALVES):
                 nc.tensor.matmul_mx(
-                    out=acc[c][h][:],
-                    lhsT=w_codes[i][:, h * P : (h + 1) * P].bitcast(FP8X4),
-                    lhsT_scale=w_scale[:, i, h * P // 4 : (h + 1) * P // 4].bitcast(U8),
-                    rhs=codes[:, cols(c)].bitcast(FP8X4),
-                    rhs_scale=scale[:, cols(c)],
+                    out=acc[i][h][:],
+                    lhsT=w_codes[:, w, h * P : (h + 1) * P].bitcast(FP8X4),
+                    lhsT_scale=w_scale[:, w, h * P // 4 : (h + 1) * P // 4].bitcast(U8),
+                    rhs=codes[:, piece(i)].bitcast(FP8X4),
+                    rhs_scale=scale[:, piece(i)],
                     start=first,
                     stop=not first,
                 )
 
-        def relu_scalar(c, h):
-            nc.scalar.activation(result[c][:, h, :], acc[c][h][:], ACT.Relu, bias=bias[h][:])
+        def relu_scalar(i, h):
+            nc.scalar.activation(result[i][:, h, :], acc[i][h][:], ACT.Relu, bias=bias[h][:])
 
-        def relu_vector(c, h):
-            nc.vector.tensor_scalar(result[c][:, h, :], acc[c][h][:], bias[h][:], 0.0, ALU.add, ALU.max)
+        def relu_vector(i, h):
+            nc.vector.tensor_scalar(result[i][:, h, :], acc[i][h][:], bias[h][:], 0.0, ALU.add, ALU.max)
 
-        def store(c):
-            nc.sync.dma_start(out=out_rows[:, :, cols(c)], in_=result[c][:])
+        def store(i):
+            nc.sync.dma_start(out=out_rows[:, :, piece(i)], in_=result[i][:])
 
-        nc.gpsimd.memset(w_scale[:], 0)
+        nc.vector.memset(w_scale[:], 0)
+        for t in (0, 1, 3):
+            nc.vector.memset(s_plane[t][:, 0:8], 0.0)
+        nc.vector.memset(w_codes[:, :, 0:8], 0)
+        nc.vector.memset(x_raw[:].rearrange("p (a j) -> p a j", j=512)[:, :, 0:8], 0.0)
         nc.vector.memset(warm[:, 0:1], 0.0)
         nc.scalar.activation(warm[:, 1:2], warm[:, 0:1], ACT.Relu)
 
         load_plane(2)
         nc.sync.dma_start(offsets[:], offs)
+        for h in range(HALVES):
+            nc.gpsimd.dma_start(out=bias[h][:], in_=b[h * P : (h + 1) * P, :])
         load_scales(1, w2_scales)
         load_plane(0)
         load_plane(1)
         load_scales(0, w1_scales)
         load_plane(3)
-        for h in range(HALVES):
-            nc.scalar.dma_start(out=bias[h][:], in_=b[h * P : (h + 1) * P, :])
-        load_x(0)
         load_codes(1, w2_words)
+        load_x(0)
         load_x(1)
         load_codes(0, w1_words)
         load_x(2)
+        load_x(3)
 
         nc.vector.tensor_copy(s_grouped[:, :, 2], s_plane[2][:].indirect(offsets[:]))
         nc.vector.tensor_copy(s_low[:, 0, :], s_plane[0][:].indirect(offsets[:]))
@@ -133,28 +148,35 @@ def tile_picked_recall_relu_e_kernel(tc, xT, sT, w1_words, w1_scales, w2_words, 
 
         nc.vector.tensor_copy(s_grouped[:, cols(0), 3], picked(3, 0))
         nc.vector.tensor_copy(s_grouped[:, cols(1), 3], picked(3, 1))
-        quantize(s_grouped, s_codes, s_scale, 0)
-        group_x(scalar_copy, 0, 0, CHUNK)
+        quantize(s_grouped, s_codes, s_scale, cols(0))
+        group_x(scalar_copy, 0)
         nc.vector.tensor_copy(s_grouped[:, cols(2), 3], picked(3, 2))
-        quantize(s_grouped, s_codes, s_scale, 1)
+        quantize(s_grouped, s_codes, s_scale, cols(1))
         multiply(1, s_codes, s_scale, 0, True)
         multiply(1, s_codes, s_scale, 1, True)
-        quantize(x_grouped, x_codes, x_scale, 0)
-        quantize(s_grouped, s_codes, s_scale, 2)
-        group_x(scalar_copy, 1, 0, CHUNK)
+        quantize(x_grouped, x_codes, x_scale, piece(0))
+        quantize(s_grouped, s_codes, s_scale, cols(2))
+        group_x(scalar_copy, 1)
         multiply(1, s_codes, s_scale, 2, True)
+        multiply(1, s_codes, s_scale, 3, True)
         multiply(0, x_codes, x_scale, 0, False)
-        quantize(x_grouped, x_codes, x_scale, 1)
+        group_x(nc.vector.tensor_copy, 2)
+        quantize(x_grouped, x_codes, x_scale, piece(1))
         multiply(0, x_codes, x_scale, 1, False)
-        group_x(nc.vector.tensor_copy, 2, 0, CHUNK)
+        quantize(x_grouped, x_codes, x_scale, piece(2))
+        multiply(0, x_codes, x_scale, 2, False)
         for h in range(HALVES):
             relu_scalar(0, h)
         store(0)
-        quantize(x_grouped, x_codes, x_scale, 2)
-        multiply(0, x_codes, x_scale, 2, False)
+        group_x(nc.vector.tensor_copy, 3)
+        quantize(x_grouped, x_codes, x_scale, piece(3))
+        multiply(0, x_codes, x_scale, 3, False)
         for h in range(HALVES):
             relu_scalar(1, h)
         store(1)
         relu_vector(2, 0)
-        relu_scalar(2, 1)
+        relu_vector(2, 1)
         store(2)
+        relu_vector(3, 0)
+        relu_scalar(3, 1)
+        store(3)

@@ -1,6 +1,7 @@
 from contextlib import ExitStack
 
 import concourse.mybir as mybir
+from concourse.masks import make_identity
 
 K, T, S, N = 512, 2048, 768, 256
 FLOPS = 2 * 2 * K * N * S
@@ -37,7 +38,9 @@ def tile_picked_recall_relu_e_kernel(tc, xT, sT, w1_words, w1_scales, w2_words, 
         x_raw = keep.tile([P, PACK * S], F32, name="x_raw")
         w_codes = keep.tile([P, 2, N], I32, name="w_codes", align_bytes=64)
         w_scale = keep.tile([P, 2, SCALE_WORDS], I32, name="w_scale", align_bytes=64)
-        bias = [keep.tile([P, 1], F32, name=f"bias{h}") for h in range(HALVES)]
+        bias_rows = keep.tile([P, P], F32, name="bias_rows")
+        bias = keep.tile([P, HALVES], F32, name="bias")
+        identity = keep.tile([P, P], F32, name="identity")
         warm = keep.tile([P, 2], F32, name="warm")
         s_low = keep.tile([P, 2, S], F32, name="s_low")
         s_grouped = keep.tile([P, S, PACK], BF16, name="s_grouped", align_bytes=64)
@@ -47,7 +50,9 @@ def tile_picked_recall_relu_e_kernel(tc, xT, sT, w1_words, w1_scales, w2_words, 
         s_scale = keep.tile([P, S], U8, name="s_scale", align_bytes=64)
         x_scale = keep.tile([P, S], U8, name="x_scale", align_bytes=64)
         result = [keep.tile([P, HALVES, z - a], F32, name=f"result{i}") for i, (a, z) in enumerate(X_PIECES)]
-        acc = [[psum.tile([P, z - a], F32, name=f"acc{i}_{h}") for h in range(HALVES)] for i, (a, z) in enumerate(X_PIECES)]
+        bias_turned = psum.tile([P, P], F32, name="bias_turned", tag="bank3_1")
+        spare = psum.tile([P, N], F32, name="spare", tag="bank3_0")
+        acc = {}
 
         s_rows = sT.rearrange("(p t) j -> t p j", t=PACK)
         x_rows = xT.rearrange("(p t) j -> p t j", t=PACK)
@@ -72,10 +77,10 @@ def tile_picked_recall_relu_e_kernel(tc, xT, sT, w1_words, w1_scales, w2_words, 
         def load_codes(w, words):
             nc.sync.dma_start(out=w_codes[:, w, :], in_=words[0].rearrange("p m r -> p (m r)").bitcast(I32))
 
-        def load_scales(w, scales):
+        def load_scales(queue, w, scales):
             rows = scales[0].bitcast(I32)
             for q in range(4):
-                nc.sync.dma_start(out=w_scale[32 * q : 32 * q + 4, w, :], in_=rows[4 * q : 4 * q + 4, :])
+                queue.dma_start(out=w_scale[32 * q : 32 * q + 4, w, :], in_=rows[4 * q : 4 * q + 4, :])
 
         def picked(t, c):
             return s_plane[t][:].indirect(offsets[:, c * (CHUNK // 16) : (c + 1) * (CHUNK // 16)])
@@ -97,8 +102,11 @@ def tile_picked_recall_relu_e_kernel(tc, xT, sT, w1_words, w1_scales, w2_words, 
 
         def multiply(w, codes, scale, i, first):
             for h in range(HALVES):
+                if first:
+                    a, z = X_PIECES[i]
+                    acc[i, h] = psum.tile([P, z - a], F32, name=f"acc{i}_{h}", tag=f"bank{i}_{h}")
                 nc.tensor.matmul_mx(
-                    out=acc[i][h][:],
+                    out=acc[i, h][:],
                     lhsT=w_codes[:, w, h * P : (h + 1) * P].bitcast(FP8X4),
                     lhsT_scale=w_scale[:, w, h * P // 4 : (h + 1) * P // 4].bitcast(U8),
                     rhs=codes[:, piece(i)].bitcast(FP8X4),
@@ -108,37 +116,41 @@ def tile_picked_recall_relu_e_kernel(tc, xT, sT, w1_words, w1_scales, w2_words, 
                 )
 
         def relu_scalar(i, h):
-            nc.scalar.activation(result[i][:, h, :], acc[i][h][:], ACT.Relu, bias=bias[h][:])
+            nc.scalar.activation(result[i][:, h, :], acc[i, h][:], ACT.Relu, bias=bias[:, h : h + 1])
 
         def relu_vector(i, h):
-            nc.vector.tensor_scalar(result[i][:, h, :], acc[i][h][:], bias[h][:], 0.0, ALU.add, ALU.max)
+            nc.vector.tensor_scalar(result[i][:, h, :], acc[i, h][:], bias[:, h : h + 1], 0.0, ALU.add, ALU.max)
 
         def store(i):
             nc.sync.dma_start(out=out_rows[:, :, piece(i)], in_=result[i][:])
 
+        nc.vector.memset(bias_rows[:], 0.0)
         nc.vector.memset(w_scale[:], 0)
-        for t in (0, 1, 3):
+        for t in (1, 3):
             nc.vector.memset(s_plane[t][:, 0:8], 0.0)
-        nc.vector.memset(w_codes[:, :, 0:8], 0)
         nc.vector.memset(x_raw[:].rearrange("p (a j) -> p a j", j=512)[:, :, 0:8], 0.0)
+        nc.vector.memset(w_codes[:, :, 0:8], 0)
         nc.vector.memset(warm[:, 0:1], 0.0)
         nc.scalar.activation(warm[:, 1:2], warm[:, 0:1], ACT.Relu)
+        make_identity(nc, identity[:])
 
         load_plane(2)
         nc.sync.dma_start(offsets[:], offs)
-        for h in range(HALVES):
-            nc.gpsimd.dma_start(out=bias[h][:], in_=b[h * P : (h + 1) * P, :])
-        load_scales(1, w2_scales)
         load_plane(0)
+        nc.sync.dma_start(out=bias_rows[0:HALVES, :], in_=b.rearrange("(h p) o -> h (p o)", p=P))
+        load_scales(nc.sync, 1, w2_scales)
+        load_scales(nc.gpsimd, 0, w1_scales)
         load_plane(1)
-        load_scales(0, w1_scales)
         load_plane(3)
-        load_codes(1, w2_words)
         load_x(0)
+        load_codes(1, w2_words)
         load_x(1)
         load_codes(0, w1_words)
         load_x(2)
         load_x(3)
+
+        nc.tensor.transpose(bias_turned[:], bias_rows[:], identity[:])
+        scalar_copy(bias[:], bias_turned[:, 0:HALVES])
 
         nc.vector.tensor_copy(s_grouped[:, :, 2], s_plane[2][:].indirect(offsets[:]))
         nc.vector.tensor_copy(s_low[:, 0, :], s_plane[0][:].indirect(offsets[:]))
@@ -150,32 +162,42 @@ def tile_picked_recall_relu_e_kernel(tc, xT, sT, w1_words, w1_scales, w2_words, 
         nc.vector.tensor_copy(s_grouped[:, cols(1), 3], picked(3, 1))
         quantize(s_grouped, s_codes, s_scale, cols(0))
         group_x(scalar_copy, 0)
+        for repeat in range(3):
+            nc.tensor.matmul_mx(
+                out=spare[:],
+                lhsT=w_codes[:, 1, 0:P].bitcast(FP8X4),
+                lhsT_scale=w_scale[:, 1, 0 : P // 4].bitcast(U8),
+                rhs=w_codes[:, 1, :].bitcast(FP8X4),
+                rhs_scale=w_scale[:, 1, :].bitcast(U8),
+                start=True,
+                stop=True,
+            )
+        multiply(1, s_codes, s_scale, 0, True)
         nc.vector.tensor_copy(s_grouped[:, cols(2), 3], picked(3, 2))
         quantize(s_grouped, s_codes, s_scale, cols(1))
-        multiply(1, s_codes, s_scale, 0, True)
         multiply(1, s_codes, s_scale, 1, True)
         quantize(x_grouped, x_codes, x_scale, piece(0))
+        multiply(0, x_codes, x_scale, 0, False)
         quantize(s_grouped, s_codes, s_scale, cols(2))
         group_x(scalar_copy, 1)
         multiply(1, s_codes, s_scale, 2, True)
         multiply(1, s_codes, s_scale, 3, True)
-        multiply(0, x_codes, x_scale, 0, False)
         group_x(nc.vector.tensor_copy, 2)
         quantize(x_grouped, x_codes, x_scale, piece(1))
         multiply(0, x_codes, x_scale, 1, False)
-        quantize(x_grouped, x_codes, x_scale, piece(2))
-        multiply(0, x_codes, x_scale, 2, False)
         for h in range(HALVES):
             relu_scalar(0, h)
         store(0)
         group_x(nc.vector.tensor_copy, 3)
+        quantize(x_grouped, x_codes, x_scale, piece(2))
+        multiply(0, x_codes, x_scale, 2, False)
         quantize(x_grouped, x_codes, x_scale, piece(3))
         multiply(0, x_codes, x_scale, 3, False)
-        for h in range(HALVES):
-            relu_scalar(1, h)
+        relu_scalar(1, 0)
+        relu_vector(1, 1)
         store(1)
         relu_vector(2, 0)
-        relu_vector(2, 1)
+        relu_scalar(2, 1)
         store(2)
         relu_vector(3, 0)
         relu_scalar(3, 1)

@@ -23,36 +23,37 @@ CHUNKS = S // CHUNK
 HALVES = N // P
 SCALE_WORDS = N // 4
 
-
-X_PIECES = ((0, 256), (256, 512), (512, 640), (640, 768))
+PIECES = ((0, 256), (256, 512), (512, 640), (640, 768))
+PLANE_BYTES = 4 * T
 
 
 def tile_picked_recall_relu_e_kernel(tc, xT, sT, w1_words, w1_scales, w2_words, w2_scales, b, offs, out):
     nc = tc.nc
     with ExitStack() as ctx:
         keep = ctx.enter_context(tc.tile_pool(name="keep", bufs=1))
+        reuse = ctx.enter_context(tc.tile_pool(name="reuse", bufs=1))
         psum = ctx.enter_context(tc.psum_pool(name="psum", bufs=1))
 
+        def placed(shape, dtype, name, offset):
+            return reuse.tile(shape, dtype, name=name, offset=offset, align_bytes=64)
+
         offsets = keep.tile([P, S // 16], U16, name="offsets")
-        s_plane = [keep.tile([P, T], F32, name=f"s_plane{t}") for t in range(PACK)]
-        x_raw = keep.tile([P, PACK * S], F32, name="x_raw")
-        w_codes = keep.tile([P, 2, N], I32, name="w_codes", align_bytes=64)
+        s_plane = [placed([P, T], F32, f"s_plane{t}", t * PLANE_BYTES) for t in range(PACK)]
+        grouped_at = PACK * PLANE_BYTES
+        x_grouped = [placed([P, z - a, PACK], BF16, f"x_grouped{i}", grouped_at + 2 * PACK * a) for i, (a, z) in enumerate(PIECES)]
         w_scale = keep.tile([P, 2, SCALE_WORDS], I32, name="w_scale", align_bytes=64)
         bias_rows = keep.tile([P, P], F32, name="bias_rows")
         bias = keep.tile([P, HALVES], F32, name="bias")
         identity = keep.tile([P, P], F32, name="identity")
-        warm = keep.tile([P, 2], F32, name="warm")
         s_low = keep.tile([P, 2, S], F32, name="s_low")
         s_grouped = keep.tile([P, S, PACK], BF16, name="s_grouped", align_bytes=64)
-        x_grouped = keep.tile([P, S, PACK], BF16, name="x_grouped", align_bytes=64)
-        s_codes = keep.tile([P, S], U32, name="s_codes", align_bytes=64)
+        s_codes = [keep.tile([P, CHUNK], U32, name="s_codes0", align_bytes=64)]
         x_codes = keep.tile([P, S], U32, name="x_codes", align_bytes=64)
         s_scale = keep.tile([P, S], U8, name="s_scale", align_bytes=64)
         x_scale = keep.tile([P, S], U8, name="x_scale", align_bytes=64)
-        result = [keep.tile([P, HALVES, z - a], F32, name=f"result{i}") for i, (a, z) in enumerate(X_PIECES)]
         bias_turned = psum.tile([P, P], F32, name="bias_turned", tag="bank3_1")
-        spare = psum.tile([P, N], F32, name="spare", tag="bank3_0")
         acc = {}
+        result = {}
 
         s_rows = sT.rearrange("(p t) j -> t p j", t=PACK)
         x_rows = xT.rearrange("(p t) j -> p t j", t=PACK)
@@ -62,20 +63,19 @@ def tile_picked_recall_relu_e_kernel(tc, xT, sT, w1_words, w1_scales, w2_words, 
             return slice(c * CHUNK, (c + 1) * CHUNK)
 
         def piece(i):
-            return slice(*X_PIECES[i])
+            return slice(*PIECES[i])
 
-        def x_piece(i):
-            a, z = X_PIECES[i]
-            return x_raw[:, PACK * a : PACK * z].rearrange("p (t j) -> p t j", t=PACK)
+        def width(i):
+            return PIECES[i][1] - PIECES[i][0]
+
+        def chunk_of(i):
+            return PIECES[i][0] // CHUNK
+
+        def within(i):
+            return slice(PIECES[i][0] % CHUNK, PIECES[i][0] % CHUNK + width(i))
 
         def load_plane(t):
             nc.sync.dma_start(out=s_plane[t][:], in_=s_rows[t])
-
-        def load_x(i):
-            nc.sync.dma_start(out=x_piece(i), in_=x_rows[:, :, piece(i)])
-
-        def load_codes(w, words):
-            nc.sync.dma_start(out=w_codes[:, w, :], in_=words[0].rearrange("p m r -> p (m r)").bitcast(I32))
 
         def load_scales(queue, w, scales):
             rows = scales[0].bitcast(I32)
@@ -85,35 +85,22 @@ def tile_picked_recall_relu_e_kernel(tc, xT, sT, w1_words, w1_scales, w2_words, 
         def picked(t, c):
             return s_plane[t][:].indirect(offsets[:, c * (CHUNK // 16) : (c + 1) * (CHUNK // 16)])
 
-        def group_x(copy, i):
-            src = x_piece(i).rearrange("p t (g e) -> p g t e", e=4)
-            dst = x_grouped[:, piece(i), :].rearrange("p (g e) t -> p g t e", e=4)
-            copy(dst, src)
-
         def scalar_copy(dst, src):
             nc.scalar.activation(dst, src, ACT.Copy)
 
-        def quantize(grouped, codes, scale, js):
+        def quantize_s(c):
             nc.vector.quantize_mx(
-                out=codes[:, js].bitcast(FP8X4),
-                scales=scale[:, js],
-                in_=grouped[:, js, :].rearrange("p j t -> p (j t)"),
+                out=s_codes[c][:].bitcast(FP8X4),
+                scales=s_scale[:, cols(c)],
+                in_=s_grouped[:, cols(c), :].rearrange("p j t -> p (j t)"),
             )
 
-        def multiply(w, codes, scale, i, first):
-            for h in range(HALVES):
-                if first:
-                    a, z = X_PIECES[i]
-                    acc[i, h] = psum.tile([P, z - a], F32, name=f"acc{i}_{h}", tag=f"bank{i}_{h}")
-                nc.tensor.matmul_mx(
-                    out=acc[i, h][:],
-                    lhsT=w_codes[:, w, h * P : (h + 1) * P].bitcast(FP8X4),
-                    lhsT_scale=w_scale[:, w, h * P // 4 : (h + 1) * P // 4].bitcast(U8),
-                    rhs=codes[:, piece(i)].bitcast(FP8X4),
-                    rhs_scale=scale[:, piece(i)],
-                    start=first,
-                    stop=not first,
-                )
+        def quantize_x(i):
+            nc.vector.quantize_mx(
+                out=x_codes[:, piece(i)].bitcast(FP8X4),
+                scales=x_scale[:, piece(i)],
+                in_=x_grouped[i][:].rearrange("p j t -> p (j t)"),
+            )
 
         def relu_scalar(i, h):
             nc.scalar.activation(result[i][:, h, :], acc[i, h][:], ACT.Relu, bias=bias[:, h : h + 1])
@@ -124,30 +111,18 @@ def tile_picked_recall_relu_e_kernel(tc, xT, sT, w1_words, w1_scales, w2_words, 
         def store(i):
             nc.sync.dma_start(out=out_rows[:, :, piece(i)], in_=result[i][:])
 
-        nc.vector.memset(bias_rows[:], 0.0)
         nc.vector.memset(w_scale[:], 0)
-        for t in (1, 3):
-            nc.vector.memset(s_plane[t][:, 0:8], 0.0)
-        nc.vector.memset(x_raw[:].rearrange("p (a j) -> p a j", j=512)[:, :, 0:8], 0.0)
-        nc.vector.memset(w_codes[:, :, 0:8], 0)
-        nc.vector.memset(warm[:, 0:1], 0.0)
-        nc.scalar.activation(warm[:, 1:2], warm[:, 0:1], ACT.Relu)
+        nc.vector.memset(bias_rows[:], 0.0)
         make_identity(nc, identity[:])
 
         load_plane(2)
         nc.sync.dma_start(offsets[:], offs)
         load_plane(0)
-        nc.sync.dma_start(out=bias_rows[0:HALVES, :], in_=b.rearrange("(h p) o -> h (p o)", p=P))
-        load_scales(nc.sync, 1, w2_scales)
-        load_scales(nc.gpsimd, 0, w1_scales)
         load_plane(1)
+        load_scales(nc.sync, 1, w2_scales)
         load_plane(3)
-        load_x(0)
-        load_codes(1, w2_words)
-        load_x(1)
-        load_codes(0, w1_words)
-        load_x(2)
-        load_x(3)
+        nc.gpsimd.dma_start(out=bias_rows[0:HALVES, :], in_=b.rearrange("(h p) o -> h (p o)", p=P))
+        load_scales(nc.gpsimd, 0, w1_scales)
 
         nc.tensor.transpose(bias_turned[:], bias_rows[:], identity[:])
         scalar_copy(bias[:], bias_turned[:, 0:HALVES])
@@ -158,46 +133,89 @@ def tile_picked_recall_relu_e_kernel(tc, xT, sT, w1_words, w1_scales, w2_words, 
             nc.vector.tensor_copy(s_low[:, 1, cols(c)], picked(1, c))
             scalar_copy(s_grouped[:, cols(c), 0:2], s_low[:, :, cols(c)].rearrange("p t j -> p j t"))
 
-        nc.vector.tensor_copy(s_grouped[:, cols(0), 3], picked(3, 0))
-        nc.vector.tensor_copy(s_grouped[:, cols(1), 3], picked(3, 1))
-        quantize(s_grouped, s_codes, s_scale, cols(0))
+        x_at = (2 * PLANE_BYTES, 2 * PLANE_BYTES + 3072, 2 * PLANE_BYTES + 6144, 0, 2048, 4096)
+        x_raw = [placed([P, PACK, P], F32, f"x_raw{u}", x_at[u]) for u in range(S // P)]
+        w_codes = [placed([P, N], I32, "w1_codes", 2 * PLANE_BYTES + 5120), placed([P, N], I32, "w2_codes", 2 * PLANE_BYTES + 2048)]
+
+        def load_x(i):
+            nc.sync.dma_start(out=x_raw[i][:], in_=x_rows[:, :, i * P : (i + 1) * P])
+
+        def load_codes(w, words):
+            nc.sync.dma_start(out=w_codes[w][:], in_=words[0].rearrange("p m r -> p (m r)").bitcast(I32))
+
+        def group_x(copy, i):
+            src = x_raw[i][:].rearrange("p t (g e) -> p g t e", e=4)
+            home = min(i // 2, 2) + i // 5
+            first = i * P - PIECES[home][0]
+            dst = x_grouped[home][:, first : first + P, :].rearrange("p (g e) t -> p g t e", e=4)
+            copy(dst, src)
+
+        def multiply(w, codes, scale, i, first):
+            for h in range(HALVES):
+                if first:
+                    acc[i, h] = psum.tile([P, width(i)], F32, name=f"acc{i}_{h}", tag=f"bank{i}_{h}")
+                nc.tensor.matmul_mx(
+                    out=acc[i, h][:],
+                    lhsT=w_codes[w][:, h * P : (h + 1) * P].bitcast(FP8X4),
+                    lhsT_scale=w_scale[:, w, h * P // 4 : (h + 1) * P // 4].bitcast(U8),
+                    rhs=codes.bitcast(FP8X4),
+                    rhs_scale=scale[:, piece(i)],
+                    start=first,
+                    stop=not first,
+                )
+
+        def multiply_s(i):
+            multiply(1, s_codes[chunk_of(i)][:, within(i)], s_scale, i, True)
+
+        def multiply_x(i):
+            multiply(0, x_codes[:, piece(i)], x_scale, i, False)
+
+        load_x(0)
+        load_codes(1, w2_words)
+        load_x(1)
+        load_codes(0, w1_words)
+        load_x(2)
+        load_x(3)
+        load_x(4)
+        load_x(5)
+
+        for i in (2, 3):
+            result[i] = keep.tile([P, HALVES, width(i)], F32, name=f"result{i}")
+        for c in range(CHUNKS):
+            nc.vector.tensor_copy(s_grouped[:, cols(c), 3], picked(3, c))
+        quantize_s(0)
+        multiply_s(0)
         group_x(scalar_copy, 0)
-        for repeat in range(3):
-            nc.tensor.matmul_mx(
-                out=spare[:],
-                lhsT=w_codes[:, 1, 0:P].bitcast(FP8X4),
-                lhsT_scale=w_scale[:, 1, 0 : P // 4].bitcast(U8),
-                rhs=w_codes[:, 1, :].bitcast(FP8X4),
-                rhs_scale=w_scale[:, 1, :].bitcast(U8),
-                start=True,
-                stop=True,
-            )
-        multiply(1, s_codes, s_scale, 0, True)
-        nc.vector.tensor_copy(s_grouped[:, cols(2), 3], picked(3, 2))
-        quantize(s_grouped, s_codes, s_scale, cols(1))
-        multiply(1, s_codes, s_scale, 1, True)
-        quantize(x_grouped, x_codes, x_scale, piece(0))
-        multiply(0, x_codes, x_scale, 0, False)
-        quantize(s_grouped, s_codes, s_scale, cols(2))
         group_x(scalar_copy, 1)
-        multiply(1, s_codes, s_scale, 2, True)
-        multiply(1, s_codes, s_scale, 3, True)
-        group_x(nc.vector.tensor_copy, 2)
-        quantize(x_grouped, x_codes, x_scale, piece(1))
-        multiply(0, x_codes, x_scale, 1, False)
-        for h in range(HALVES):
-            relu_scalar(0, h)
+        quantize_x(0)
+        multiply_x(0)
+        for c in (1, 2):
+            s_codes.append(placed([P, CHUNK], U32, f"s_codes{c}", grouped_at + 4 * CHUNK * (c - 1)))
+        quantize_s(1)
+        multiply_s(1)
+        quantize_s(2)
+        group_x(scalar_copy, 2)
+        group_x(scalar_copy, 3)
+        group_x(scalar_copy, 4)
+        result[0] = placed([P, HALVES, CHUNK], F32, "result0", x_at[3])
+        relu_vector(0, 0)
+        relu_scalar(0, 1)
         store(0)
-        group_x(nc.vector.tensor_copy, 3)
-        quantize(x_grouped, x_codes, x_scale, piece(2))
-        multiply(0, x_codes, x_scale, 2, False)
-        quantize(x_grouped, x_codes, x_scale, piece(3))
-        multiply(0, x_codes, x_scale, 3, False)
+        quantize_x(1)
+        multiply_x(1)
+        multiply_s(2)
+        multiply_s(3)
+        group_x(nc.vector.tensor_copy, 5)
+        quantize_x(2)
+        multiply_x(2)
+        quantize_x(3)
+        multiply_x(3)
+        result[1] = placed([P, HALVES, CHUNK], F32, "result1", x_at[4])
         relu_scalar(1, 0)
-        relu_vector(1, 1)
+        relu_scalar(1, 1)
         store(1)
         relu_vector(2, 0)
-        relu_scalar(2, 1)
+        relu_vector(2, 1)
         store(2)
         relu_vector(3, 0)
         relu_scalar(3, 1)

@@ -1,7 +1,6 @@
 from contextlib import ExitStack
 
 import concourse.mybir as mybir
-from concourse.masks import make_identity
 
 K, T, S, N = 512, 2048, 768, 256
 FLOPS = 2 * 2 * K * N * S
@@ -42,16 +41,14 @@ def tile_picked_recall_relu_e_kernel(tc, xT, sT, w1_words, w1_scales, w2_words, 
         grouped_at = PACK * PLANE_BYTES
         x_grouped = [placed([P, z - a, PACK], BF16, f"x_grouped{i}", grouped_at + 2 * PACK * a) for i, (a, z) in enumerate(PIECES)]
         w_scale = keep.tile([P, 2, SCALE_WORDS], I32, name="w_scale", align_bytes=64)
-        bias_rows = keep.tile([P, P], F32, name="bias_rows")
-        bias = keep.tile([P, HALVES], F32, name="bias")
-        identity = keep.tile([P, P], F32, name="identity")
+        bias_rows = keep.tile([P, 32], F32, name="bias_rows", align_bytes=64)
+        bias = keep.tile([P, 32], F32, name="bias", align_bytes=64)
         s_low = keep.tile([P, 2, S], F32, name="s_low")
         s_grouped = keep.tile([P, S, PACK], BF16, name="s_grouped", align_bytes=64)
         s_codes = [keep.tile([P, CHUNK], U32, name="s_codes0", align_bytes=64)]
         x_codes = keep.tile([P, S], U32, name="x_codes", align_bytes=64)
         s_scale = keep.tile([P, S], U8, name="s_scale", align_bytes=64)
         x_scale = keep.tile([P, S], U8, name="x_scale", align_bytes=64)
-        bias_turned = psum.tile([P, P], F32, name="bias_turned", tag="bank3_1")
         acc = {}
         result = {}
 
@@ -77,9 +74,9 @@ def tile_picked_recall_relu_e_kernel(tc, xT, sT, w1_words, w1_scales, w2_words, 
         def load_plane(t):
             nc.sync.dma_start(out=s_plane[t][:], in_=s_rows[t])
 
-        def load_scales(queue, w, scales):
+        def load_scales(queue, w, scales, quadrants):
             rows = scales[0].bitcast(I32)
-            for q in range(4):
+            for q in quadrants:
                 queue.dma_start(out=w_scale[32 * q : 32 * q + 4, w, :], in_=rows[4 * q : 4 * q + 4, :])
 
         def picked(t, c):
@@ -103,51 +100,56 @@ def tile_picked_recall_relu_e_kernel(tc, xT, sT, w1_words, w1_scales, w2_words, 
             )
 
         def relu_scalar(i, h):
-            nc.scalar.activation(result[i][:, h, :], acc[i, h][:], ACT.Relu, bias=bias[:, h : h + 1])
+            nc.scalar.activation(result[i, h], acc[i, h][:], ACT.Relu, bias=bias[:, h : h + 1])
 
         def relu_vector(i, h):
-            nc.vector.tensor_scalar(result[i][:, h, :], acc[i, h][:], bias[:, h : h + 1], 0.0, ALU.add, ALU.max)
+            nc.vector.tensor_scalar(result[i, h], acc[i, h][:], bias[:, h : h + 1], 0.0, ALU.add, ALU.max)
+
+        def store_half(i, h):
+            nc.sync.dma_start(out=out_rows[:, h, piece(i)], in_=result[i, h])
 
         def store(i):
-            nc.sync.dma_start(out=out_rows[:, :, piece(i)], in_=result[i][:])
+            nc.sync.dma_start(out=out_rows[:, :, piece(i)], in_=narrow[i][:])
 
         nc.vector.memset(w_scale[:], 0)
         nc.vector.memset(bias_rows[:], 0.0)
-        make_identity(nc, identity[:])
 
         load_plane(2)
         nc.sync.dma_start(offsets[:], offs)
         load_plane(0)
         load_plane(1)
-        load_scales(nc.sync, 1, w2_scales)
+        b_rows = b.rearrange("(h q c) o -> h q (c o)", h=HALVES, c=32)
+        for h in range(HALVES):
+            nc.sync.dma_start(out=bias_rows[h:P:32, :], in_=b_rows[h])
+        load_scales(nc.sync, 1, w2_scales, (0, 1, 2))
         load_plane(3)
-        nc.gpsimd.dma_start(out=bias_rows[0:HALVES, :], in_=b.rearrange("(h p) o -> h (p o)", p=P))
-        load_scales(nc.gpsimd, 0, w1_scales)
+        load_scales(nc.sync, 1, w2_scales, (3,))
+        load_scales(nc.gpsimd, 0, w1_scales, (0, 1, 2, 3))
 
-        nc.tensor.transpose(bias_turned[:], bias_rows[:], identity[:])
-        scalar_copy(bias[:], bias_turned[:, 0:HALVES])
 
         nc.vector.tensor_copy(s_grouped[:, :, 2], s_plane[2][:].indirect(offsets[:]))
         nc.vector.tensor_copy(s_low[:, 0, :], s_plane[0][:].indirect(offsets[:]))
+        nc.vector.transpose(bias[:], bias_rows[:])
         for c in range(CHUNKS):
             nc.vector.tensor_copy(s_low[:, 1, cols(c)], picked(1, c))
             scalar_copy(s_grouped[:, cols(c), 0:2], s_low[:, :, cols(c)].rearrange("p t j -> p j t"))
 
-        x_at = (2 * PLANE_BYTES, 2 * PLANE_BYTES + 3072, 2 * PLANE_BYTES + 6144, 0, 2048, 4096)
-        x_raw = [placed([P, PACK, P], F32, f"x_raw{u}", x_at[u]) for u in range(S // P)]
-        w_codes = [placed([P, N], I32, "w1_codes", 2 * PLANE_BYTES + 5120), placed([P, N], I32, "w2_codes", 2 * PLANE_BYTES + 2048)]
+        x_at = (2 * PLANE_BYTES, None, 2 * PLANE_BYTES + 6144, 0, 2048, 4096)
+        x_raw = {u: placed([P, PACK, P if u else CHUNK], F32, f"x_raw{u}", x_at[u]) for u in (0, 2, 3, 4, 5)}
+        w_both = placed([P, 2 * N], I32, "w_both", 2 * PLANE_BYTES + 4096)
+        w_codes = [w_both[:, 0:N], w_both[:, N : 2 * N]]
 
         def load_x(i):
-            nc.sync.dma_start(out=x_raw[i][:], in_=x_rows[:, :, i * P : (i + 1) * P])
+            nc.sync.dma_start(out=x_raw[i][:], in_=x_rows[:, :, i * P : (i + 1) * P if i else CHUNK])
 
         def load_codes(w, words):
-            nc.sync.dma_start(out=w_codes[w][:], in_=words[0].rearrange("p m r -> p (m r)").bitcast(I32))
+            nc.sync.dma_start(out=w_codes[w], in_=words[0].rearrange("p m r -> p (m r)").bitcast(I32))
 
         def group_x(copy, i):
             src = x_raw[i][:].rearrange("p t (g e) -> p g t e", e=4)
             home = min(i // 2, 2) + i // 5
             first = i * P - PIECES[home][0]
-            dst = x_grouped[home][:, first : first + P, :].rearrange("p (g e) t -> p g t e", e=4)
+            dst = x_grouped[home][:, first : first + (P if i else CHUNK), :].rearrange("p (g e) t -> p g t e", e=4)
             copy(dst, src)
 
         def multiply(w, codes, scale, i, first):
@@ -172,35 +174,48 @@ def tile_picked_recall_relu_e_kernel(tc, xT, sT, w1_words, w1_scales, w2_words, 
 
         load_x(0)
         load_codes(1, w2_words)
-        load_x(1)
         load_codes(0, w1_words)
         load_x(2)
         load_x(3)
         load_x(4)
         load_x(5)
 
+        spare = psum.tile([P, 2 * N], F32, name="spare", tag="bank3_0")
+        nc.tensor.matmul_mx(
+            out=spare[:],
+            lhsT=w_codes[1][:, 0:P].bitcast(FP8X4),
+            lhsT_scale=w_scale[:, 1, 0 : P // 4].bitcast(U8),
+            rhs=w_both[:].bitcast(FP8X4),
+            rhs_scale=w_scale[:].rearrange("p w n -> p (w n)").bitcast(U8),
+            start=True,
+            stop=True,
+        )
+        narrow = {i: keep.tile([P, HALVES, P], F32, name=f"narrow{i}") for i in (2, 3)}
         for i in (2, 3):
-            result[i] = keep.tile([P, HALVES, width(i)], F32, name=f"result{i}")
-        for c in range(CHUNKS):
+            for h in range(HALVES):
+                result[i, h] = narrow[i][:, h, :]
+        for c in (0, 1):
             nc.vector.tensor_copy(s_grouped[:, cols(c), 3], picked(3, c))
         quantize_s(0)
         multiply_s(0)
+        nc.vector.tensor_copy(s_grouped[:, cols(2), 3], picked(3, 2))
         group_x(scalar_copy, 0)
-        group_x(scalar_copy, 1)
         quantize_x(0)
         multiply_x(0)
         for c in (1, 2):
-            s_codes.append(placed([P, CHUNK], U32, f"s_codes{c}", grouped_at + 4 * CHUNK * (c - 1)))
+            s_codes.append(placed([P, CHUNK], U32, f"s_codes{c}", x_at[0] + 4 * CHUNK * (c - 1)))
         quantize_s(1)
         multiply_s(1)
         quantize_s(2)
         group_x(scalar_copy, 2)
         group_x(scalar_copy, 3)
         group_x(scalar_copy, 4)
-        result[0] = placed([P, HALVES, CHUNK], F32, "result0", x_at[3])
+        result[0, 0] = keep.tile([P, CHUNK], F32, name="result0_0")[:]
         relu_vector(0, 0)
+        store_half(0, 0)
+        result[0, 1] = placed([P, CHUNK], F32, "result0_1", x_at[4] - 768)[:]
         relu_scalar(0, 1)
-        store(0)
+        store_half(0, 1)
         quantize_x(1)
         multiply_x(1)
         multiply_s(2)
@@ -210,10 +225,10 @@ def tile_picked_recall_relu_e_kernel(tc, xT, sT, w1_words, w1_scales, w2_words, 
         multiply_x(2)
         quantize_x(3)
         multiply_x(3)
-        result[1] = placed([P, HALVES, CHUNK], F32, "result1", x_at[4])
-        relu_scalar(1, 0)
-        relu_scalar(1, 1)
-        store(1)
+        for h in range(HALVES):
+            result[1, h] = placed([P, CHUNK], F32, f"result1_{h}", x_at[4] + 256 + 4 * CHUNK * h)[:]
+            relu_scalar(1, h)
+            store_half(1, h)
         relu_vector(2, 0)
         relu_vector(2, 1)
         store(2)

@@ -202,36 +202,31 @@ def tile_picked_recall_relu_e_kernel(tc, xT, sT, w1_words, w1_scales, w2_words, 
         group_x(scalar_copy, 0)
         quantize_x(0)
         multiply_x(0)
-        for c in (1, 2):
-            s_codes.append(placed([P, CHUNK], U32, f"s_codes{c}", x_at[0] + 4 * CHUNK * (c - 1)))
+        s_codes.append(placed([P, CHUNK], U32, "s_codes1", x_at[0]))
         quantize_s(1)
         multiply_s(1)
-        quantize_s(2)
         group_x(scalar_copy, 2)
         group_x(scalar_copy, 3)
-        group_x(scalar_copy, 4)
-        result[0, 0] = keep.tile([P, CHUNK], F32, name="result0_0")[:]
-        relu_vector(0, 0)
-        store_half(0, 0)
-        result[0, 1] = placed([P, CHUNK], F32, "result0_1", x_at[4] - 768)[:]
-        relu_scalar(0, 1)
-        store_half(0, 1)
         quantize_x(1)
         multiply_x(1)
+        s_codes.append(placed([P, CHUNK], U32, "s_codes2", x_at[3]))
+        quantize_s(2)
         multiply_s(2)
         multiply_s(3)
+        group_x(scalar_copy, 4)
         group_x(nc.vector.tensor_copy, 5)
         quantize_x(2)
         multiply_x(2)
         quantize_x(3)
         multiply_x(3)
-        for h in range(HALVES):
-            result[1, h] = placed([P, CHUNK], F32, f"result1_{h}", x_at[4] + 256 + 4 * CHUNK * h)[:]
-            relu_scalar(1, h)
-            store_half(1, h)
-        relu_vector(2, 0)
-        relu_vector(2, 1)
-        store(2)
-        relu_vector(3, 0)
-        relu_scalar(3, 1)
-        store(3)
+        for u, (i, h) in enumerate(((0, 0), (0, 1), (1, 0))):
+            result[i, h] = placed([P, CHUNK], F32, f"result{i}_{h}", x_at[4] - 768 + 4 * CHUNK * u)[:]
+            relu_scalar(i, h)
+            store_half(i, h)
+        result[1, 1] = placed([P, CHUNK], F32, "result1_1", grouped_at + 2 * PACK * PIECES[3][0])[:]
+        relu_vector(1, 1)
+        store_half(1, 1)
+        for i in (2, 3):
+            relu_vector(i, 0)
+            relu_scalar(i, 1)
+            store(i)

@@ -207,26 +207,25 @@ def tile_picked_recall_relu_e_kernel(tc, xT, sT, w1_words, w1_scales, w2_words, 
         multiply_s(1)
         group_x(scalar_copy, 2)
         group_x(scalar_copy, 3)
+        group_x(nc.vector.tensor_copy, 4)
         quantize_x(1)
         multiply_x(1)
         s_codes.append(placed([P, CHUNK], U32, "s_codes2", x_at[3]))
         quantize_s(2)
         multiply_s(2)
         multiply_s(3)
-        group_x(scalar_copy, 4)
         group_x(nc.vector.tensor_copy, 5)
         quantize_x(2)
         multiply_x(2)
         quantize_x(3)
         multiply_x(3)
-        for u, (i, h) in enumerate(((0, 0), (0, 1), (1, 0))):
-            result[i, h] = placed([P, CHUNK], F32, f"result{i}_{h}", x_at[4] - 768 + 4 * CHUNK * u)[:]
+        for u, (i, h) in enumerate(((0, 0), (0, 1), (1, 0), (1, 1))):
+            result[i, h] = placed([P, CHUNK], F32, f"result{i}_{h}", x_at[3] + 4 * CHUNK * (u + 1))[:]
             relu_scalar(i, h)
             store_half(i, h)
-        result[1, 1] = placed([P, CHUNK], F32, "result1_1", grouped_at + 2 * PACK * PIECES[3][0])[:]
-        relu_vector(1, 1)
-        store_half(1, 1)
-        for i in (2, 3):
-            relu_vector(i, 0)
-            relu_scalar(i, 1)
-            store(i)
+        relu_vector(2, 0)
+        relu_vector(2, 1)
+        store(2)
+        relu_vector(3, 0)
+        relu_scalar(3, 1)
+        store(3)

@@ -180,16 +180,6 @@ def tile_picked_recall_relu_e_kernel(tc, xT, sT, w1_words, w1_scales, w2_words, 
         load_x(4)
         load_x(5)
 
-        spare = psum.tile([P, 2 * N], F32, name="spare", tag="bank3_0")
-        nc.tensor.matmul_mx(
-            out=spare[:],
-            lhsT=w_codes[1][:, 0:P].bitcast(FP8X4),
-            lhsT_scale=w_scale[:, 1, 0 : P // 4].bitcast(U8),
-            rhs=w_both[:].bitcast(FP8X4),
-            rhs_scale=w_scale[:].rearrange("p w n -> p (w n)").bitcast(U8),
-            start=True,
-            stop=True,
-        )
         narrow = {i: keep.tile([P, HALVES, P], F32, name=f"narrow{i}") for i in (2, 3)}
         for i in (2, 3):
             for h in range(HALVES):

@@ -44,7 +44,9 @@ def tile_picked_recall_relu_e_kernel(tc, xT, sT, w1_words, w1_scales, w2_words, 
         bias_rows = keep.tile([P, 32], F32, name="bias_rows", align_bytes=64)
         bias = keep.tile([P, 32], F32, name="bias", align_bytes=64)
         s_low = keep.tile([P, 2, S], F32, name="s_low")
-        s_grouped = keep.tile([P, S, PACK], BF16, name="s_grouped", align_bytes=64)
+        s_outer = keep.tile([P, 4, P, PACK], BF16, name="s_outer", align_bytes=64)
+        s_middle = keep.tile([P, 2, P, PACK], BF16, name="s_middle", align_bytes=64)
+        s_grouped = [s_outer[:, 1:3], s_middle[:], s_outer[:, 0:4:3]]
         s_codes = [keep.tile([P, CHUNK], U32, name="s_codes0", align_bytes=64)]
         x_codes = keep.tile([P, S], U32, name="x_codes", align_bytes=64)
         s_scale = keep.tile([P, S], U8, name="s_scale", align_bytes=64)
@@ -86,11 +88,19 @@ def tile_picked_recall_relu_e_kernel(tc, xT, sT, w1_words, w1_scales, w2_words, 
             nc.scalar.activation(dst, src, ACT.Copy)
 
         def quantize_s(c):
-            nc.vector.quantize_mx(
-                out=s_codes[c][:].bitcast(FP8X4),
-                scales=s_scale[:, cols(c)],
-                in_=s_grouped[:, cols(c), :].rearrange("p j t -> p (j t)"),
-            )
+            if c < 2:
+                nc.vector.quantize_mx(
+                    out=s_codes[c][:].bitcast(FP8X4),
+                    scales=s_scale[:, cols(c)],
+                    in_=s_grouped[c].rearrange("p u j t -> p (u j t)"),
+                )
+            else:
+                for u in range(2):
+                    nc.vector.quantize_mx(
+                        out=s_codes[c][:, u * P : (u + 1) * P].bitcast(FP8X4),
+                        scales=s_scale[:, c * CHUNK + u * P : c * CHUNK + (u + 1) * P],
+                        in_=s_grouped[c][:, u].rearrange("p j t -> p (j t)"),
+                    )
 
         def quantize_x(i):
             nc.vector.quantize_mx(
@@ -127,12 +137,13 @@ def tile_picked_recall_relu_e_kernel(tc, xT, sT, w1_words, w1_scales, w2_words, 
         load_scales(nc.gpsimd, 0, w1_scales, (0, 1, 2, 3))
 
 
-        nc.vector.tensor_copy(s_grouped[:, :, 2], s_plane[2][:].indirect(offsets[:]))
+        for c in range(CHUNKS):
+            nc.vector.tensor_copy(s_grouped[c][:, :, :, 2], picked(2, c))
         nc.vector.tensor_copy(s_low[:, 0, :], s_plane[0][:].indirect(offsets[:]))
         nc.vector.transpose(bias[:], bias_rows[:])
-        for c in range(CHUNKS):
+        for c in (2, 0, 1):
             nc.vector.tensor_copy(s_low[:, 1, cols(c)], picked(1, c))
-            scalar_copy(s_grouped[:, cols(c), 0:2], s_low[:, :, cols(c)].rearrange("p t j -> p j t"))
+            scalar_copy(s_grouped[c][:, :, :, 0:2], s_low[:, :, cols(c)].rearrange("p t (u j) -> p u j t", u=2))
 
         x_at = (2 * PLANE_BYTES, None, 2 * PLANE_BYTES + 6144, 0, 2048, 4096)
         x_raw = {u: placed([P, PACK, P if u else CHUNK], F32, f"x_raw{u}", x_at[u]) for u in (0, 2, 3, 4, 5)}
@@ -185,16 +196,16 @@ def tile_picked_recall_relu_e_kernel(tc, xT, sT, w1_words, w1_scales, w2_words, 
             for h in range(HALVES):
                 result[i, h] = narrow[i][:, h, :]
         for c in (0, 1):
-            nc.vector.tensor_copy(s_grouped[:, cols(c), 3], picked(3, c))
+            nc.vector.tensor_copy(s_grouped[c][:, :, :, 3], picked(3, c))
         quantize_s(0)
         multiply_s(0)
-        nc.vector.tensor_copy(s_grouped[:, cols(2), 3], picked(3, 2))
+        s_codes.append(keep.tile([P, CHUNK], U32, name="s_codes1", align_bytes=64))
+        quantize_s(1)
+        multiply_s(1)
+        nc.vector.tensor_copy(s_grouped[2][:, :, :, 3], picked(3, 2))
         group_x(scalar_copy, 0)
         quantize_x(0)
         multiply_x(0)
-        s_codes.append(placed([P, CHUNK], U32, "s_codes1", x_at[0]))
-        quantize_s(1)
-        multiply_s(1)
         group_x(scalar_copy, 2)
         group_x(scalar_copy, 3)
         group_x(nc.vector.tensor_copy, 4)

@@ -199,7 +199,7 @@ def tile_picked_recall_relu_e_kernel(tc, xT, sT, w1_words, w1_scales, w2_words, 
             nc.vector.tensor_copy(s_grouped[c][:, :, :, 3], picked(3, c))
         quantize_s(0)
         multiply_s(0)
-        s_codes.append(keep.tile([P, CHUNK], U32, name="s_codes1", align_bytes=64))
+        s_codes.append(placed([P, CHUNK], U32, "s_codes1", PLANE_BYTES))
         quantize_s(1)
         multiply_s(1)
         nc.vector.tensor_copy(s_grouped[2][:, :, :, 3], picked(3, 2))

@@ -23,7 +23,8 @@ HALVES = N // P
 SCALE_WORDS = N // 4
 
 PIECES = ((0, 256), (256, 512), (512, 640), (640, 768))
-PLANE_BYTES = 4 * T
+KIB = 1024
+PLANE_AT = (8 * KIB, 32 * KIB, 0, 24 * KIB)
 
 
 def tile_picked_recall_relu_e_kernel(tc, xT, sT, w1_words, w1_scales, w2_words, w2_scales, b, offs, out):
@@ -33,24 +34,24 @@ def tile_picked_recall_relu_e_kernel(tc, xT, sT, w1_words, w1_scales, w2_words, 
         reuse = ctx.enter_context(tc.tile_pool(name="reuse", bufs=1))
         psum = ctx.enter_context(tc.psum_pool(name="psum", bufs=1))
 
-        def placed(shape, dtype, name, offset):
-            return reuse.tile(shape, dtype, name=name, offset=offset, align_bytes=64)
+        def placed(shape, dtype, name, offset, align=64):
+            return reuse.tile(shape, dtype, name=name, offset=offset, align_bytes=align)
 
         offsets = keep.tile([P, S // 16], U16, name="offsets")
-        s_plane = [placed([P, T], F32, f"s_plane{t}", t * PLANE_BYTES) for t in range(PACK)]
-        grouped_at = PACK * PLANE_BYTES
+        s_plane = [placed([P, T], F32, f"s_plane{t}", PLANE_AT[t], 64 if PLANE_AT[t] else 64 * KIB) for t in range(PACK)]
+        grouped_at = 40 * KIB
         x_grouped = [placed([P, z - a, PACK], BF16, f"x_grouped{i}", grouped_at + 2 * PACK * a) for i, (a, z) in enumerate(PIECES)]
-        w_scale = keep.tile([P, 2, SCALE_WORDS], I32, name="w_scale", align_bytes=64)
-        bias_rows = keep.tile([P, 32], F32, name="bias_rows", align_bytes=64)
-        bias = keep.tile([P, 32], F32, name="bias", align_bytes=64)
-        s_low = keep.tile([P, 2, S], F32, name="s_low")
-        s_outer = keep.tile([P, 4, P, PACK], BF16, name="s_outer", align_bytes=64)
-        s_middle = keep.tile([P, 2, P, PACK], BF16, name="s_middle", align_bytes=64)
+        w_scale = placed([P, 2, SCALE_WORDS], I32, "w_scale", 70 * KIB)
+        bias_rows = placed([P, 32], F32, "bias_rows", 71 * KIB)
+        bias = placed([P, 32], F32, "bias", 71 * KIB + 128)
+        s_low = placed([P, 2, S], F32, "s_low", 72 * KIB)
+        s_outer = placed([P, 4, P, PACK], BF16, "s_outer", 48 * KIB)
+        s_middle = placed([P, 2, P, PACK], BF16, "s_middle", 52 * KIB)
         s_grouped = [s_outer[:, 1:3], s_middle[:], s_outer[:, 0:4:3]]
-        s_codes = [keep.tile([P, CHUNK], U32, name="s_codes0", align_bytes=64)]
-        x_codes = keep.tile([P, S], U32, name="x_codes", align_bytes=64)
-        s_scale = keep.tile([P, S], U8, name="s_scale", align_bytes=64)
-        x_scale = keep.tile([P, S], U8, name="x_scale", align_bytes=64)
+        s_codes = [placed([P, CHUNK], U32, "s_codes0", 64 * KIB)]
+        x_codes = placed([P, S], U32, "x_codes", 65 * KIB)
+        s_scale = placed([P, S], U8, "s_scale", 46 * KIB)
+        x_scale = placed([P, S], U8, "x_scale", 47 * KIB)
         acc = {}
         result = {}
 
@@ -145,9 +146,9 @@ def tile_picked_recall_relu_e_kernel(tc, xT, sT, w1_words, w1_scales, w2_words, 
             nc.vector.tensor_copy(s_low[:, 1, cols(c)], picked(1, c))
             scalar_copy(s_grouped[c][:, :, :, 0:2], s_low[:, :, cols(c)].rearrange("p t (u j) -> p u j t", u=2))
 
-        x_at = (2 * PLANE_BYTES, None, 2 * PLANE_BYTES + 6144, 0, 2048, 4096)
+        x_at = (PLANE_AT[2], None, PLANE_AT[2] + 6144, PLANE_AT[0], PLANE_AT[0] + 2048, PLANE_AT[0] + 4096)
         x_raw = {u: placed([P, PACK, P if u else CHUNK], F32, f"x_raw{u}", x_at[u]) for u in (0, 2, 3, 4, 5)}
-        w_both = placed([P, 2 * N], I32, "w_both", 2 * PLANE_BYTES + 4096)
+        w_both = placed([P, 2 * N], I32, "w_both", PLANE_AT[2] + 4096)
         w_codes = [w_both[:, 0:N], w_both[:, N : 2 * N]]
 
         def load_x(i):
@@ -191,7 +192,7 @@ def tile_picked_recall_relu_e_kernel(tc, xT, sT, w1_words, w1_scales, w2_words, 
         load_x(4)
         load_x(5)
 
-        narrow = {i: keep.tile([P, HALVES, P], F32, name=f"narrow{i}") for i in (2, 3)}
+        narrow = {i: placed([P, HALVES, P], F32, f"narrow{i}", (66 + i) * KIB) for i in (2, 3)}
         for i in (2, 3):
             for h in range(HALVES):
                 result[i, h] = narrow[i][:, h, :]
@@ -199,7 +200,7 @@ def tile_picked_recall_relu_e_kernel(tc, xT, sT, w1_words, w1_scales, w2_words, 
             nc.vector.tensor_copy(s_grouped[c][:, :, :, 3], picked(3, c))
         quantize_s(0)
         multiply_s(0)
-        s_codes.append(placed([P, CHUNK], U32, "s_codes1", PLANE_BYTES))
+        s_codes.append(placed([P, CHUNK], U32, "s_codes1", PLANE_AT[1]))
         quantize_s(1)
         multiply_s(1)
         nc.vector.tensor_copy(s_grouped[2][:, :, :, 3], picked(3, 2))

@@ -208,11 +208,11 @@ def tile_picked_recall_relu_e_kernel(tc, xT, sT, w1_words, w1_scales, w2_words, 
         quantize_x(0)
         multiply_x(0)
         group_x(scalar_copy, 2)
-        group_x(scalar_copy, 3)
-        group_x(nc.vector.tensor_copy, 4)
+        group_x(nc.vector.tensor_copy, 3)
+        group_x(scalar_copy, 4)
         quantize_x(1)
         multiply_x(1)
-        s_codes.append(placed([P, CHUNK], U32, "s_codes2", x_at[3]))
+        s_codes.append(placed([P, CHUNK], U32, "s_codes2", x_at[2]))
         quantize_s(2)
         multiply_s(2)
         multiply_s(3)
@@ -222,7 +222,7 @@ def tile_picked_recall_relu_e_kernel(tc, xT, sT, w1_words, w1_scales, w2_words, 
         quantize_x(3)
         multiply_x(3)
         for u, (i, h) in enumerate(((0, 0), (0, 1), (1, 0), (1, 1))):
-            result[i, h] = placed([P, CHUNK], F32, f"result{i}_{h}", x_at[3] + 4 * CHUNK * (u + 1))[:]
+            result[i, h] = placed([P, CHUNK], F32, f"result{i}_{h}", 48 * KIB + 4 * CHUNK * u)[:]
             relu_scalar(i, h)
             store_half(i, h)
         relu_vector(2, 0)

@@ -24,7 +24,7 @@ SCALE_WORDS = N // 4
 
 PIECES = ((0, 256), (256, 512), (512, 640), (640, 768))
 KIB = 1024
-PLANE_AT = (8 * KIB, 32 * KIB, 0, 24 * KIB)
+PLANE_AT = (0, 8 * KIB, 32 * KIB, 24 * KIB)
 
 
 def tile_picked_recall_relu_e_kernel(tc, xT, sT, w1_words, w1_scales, w2_words, w2_scales, b, offs, out):
@@ -45,6 +45,7 @@ def tile_picked_recall_relu_e_kernel(tc, xT, sT, w1_words, w1_scales, w2_words, 
         bias_rows = placed([P, 32], F32, "bias_rows", 71 * KIB)
         bias = placed([P, 32], F32, "bias", 71 * KIB + 128)
         s_low = placed([P, 2, S], F32, "s_low", 72 * KIB)
+        s_high = placed([P, 2, CHUNK], F32, "s_high", 78 * KIB)
         s_outer = placed([P, 4, P, PACK], BF16, "s_outer", 48 * KIB)
         s_middle = placed([P, 2, P, PACK], BF16, "s_middle", 52 * KIB)
         s_grouped = [s_outer[:, 1:3], s_middle[:], s_outer[:, 0:4:3]]
@@ -125,10 +126,10 @@ def tile_picked_recall_relu_e_kernel(tc, xT, sT, w1_words, w1_scales, w2_words, 
         nc.vector.memset(w_scale[:], 0)
         nc.vector.memset(bias_rows[:], 0.0)
 
-        load_plane(2)
-        nc.sync.dma_start(offsets[:], offs)
         load_plane(0)
+        nc.sync.dma_start(offsets[:], offs)
         load_plane(1)
+        load_plane(2)
         b_rows = b.rearrange("(h q c) o -> h q (c o)", h=HALVES, c=32)
         for h in range(HALVES):
             nc.sync.dma_start(out=bias_rows[h:P:32, :], in_=b_rows[h])
@@ -138,17 +139,18 @@ def tile_picked_recall_relu_e_kernel(tc, xT, sT, w1_words, w1_scales, w2_words, 
         load_scales(nc.gpsimd, 0, w1_scales, (0, 1, 2, 3))
 
 
-        for c in range(CHUNKS):
-            nc.vector.tensor_copy(s_grouped[c][:, :, :, 2], picked(2, c))
         nc.vector.tensor_copy(s_low[:, 0, :], s_plane[0][:].indirect(offsets[:]))
-        nc.vector.transpose(bias[:], bias_rows[:])
-        for c in (2, 0, 1):
+        for c in range(CHUNKS):
             nc.vector.tensor_copy(s_low[:, 1, cols(c)], picked(1, c))
             scalar_copy(s_grouped[c][:, :, :, 0:2], s_low[:, :, cols(c)].rearrange("p t (u j) -> p u j t", u=2))
+        nc.vector.transpose(bias[:], bias_rows[:])
+        for c in (0, 1):
+            nc.vector.tensor_copy(s_grouped[c][:, :, :, 2], picked(2, c))
+        scalar_copy(s_high[:, 0, :], picked(2, 2))
 
-        x_at = (PLANE_AT[2], None, PLANE_AT[2] + 6144, PLANE_AT[0], PLANE_AT[0] + 2048, PLANE_AT[0] + 4096)
+        x_at = (PLANE_AT[0], None, PLANE_AT[0] + 6144, PLANE_AT[1], PLANE_AT[1] + 2048, PLANE_AT[1] + 4096)
         x_raw = {u: placed([P, PACK, P if u else CHUNK], F32, f"x_raw{u}", x_at[u]) for u in (0, 2, 3, 4, 5)}
-        w_both = placed([P, 2 * N], I32, "w_both", PLANE_AT[2] + 4096)
+        w_both = placed([P, 2 * N], I32, "w_both", PLANE_AT[0] + 4096)
         w_codes = [w_both[:, 0:N], w_both[:, N : 2 * N]]
 
         def load_x(i):
@@ -157,12 +159,12 @@ def tile_picked_recall_relu_e_kernel(tc, xT, sT, w1_words, w1_scales, w2_words, 
         def load_codes(w, words):
             nc.sync.dma_start(out=w_codes[w], in_=words[0].rearrange("p m r -> p (m r)").bitcast(I32))
 
-        def group_x(copy, i):
+        def group_x(copy, i, part=slice(None)):
             src = x_raw[i][:].rearrange("p t (g e) -> p g t e", e=4)
             home = min(i // 2, 2) + i // 5
             first = i * P - PIECES[home][0]
             dst = x_grouped[home][:, first : first + (P if i else CHUNK), :].rearrange("p (g e) t -> p g t e", e=4)
-            copy(dst, src)
+            copy(dst[:, part], src[:, part])
 
         def multiply(w, codes, scale, i, first):
             for h in range(HALVES):
@@ -198,12 +200,13 @@ def tile_picked_recall_relu_e_kernel(tc, xT, sT, w1_words, w1_scales, w2_words, 
                 result[i, h] = narrow[i][:, h, :]
         for c in (0, 1):
             nc.vector.tensor_copy(s_grouped[c][:, :, :, 3], picked(3, c))
+        scalar_copy(s_high[:, 1, :], picked(3, 2))
         quantize_s(0)
         multiply_s(0)
-        s_codes.append(placed([P, CHUNK], U32, "s_codes1", PLANE_AT[1]))
+        s_codes.append(placed([P, CHUNK], U32, "s_codes1", PLANE_AT[2]))
         quantize_s(1)
         multiply_s(1)
-        nc.vector.tensor_copy(s_grouped[2][:, :, :, 3], picked(3, 2))
+        nc.vector.tensor_copy(s_grouped[2][:, :, :, 2:4], s_high[:].rearrange("p t (u j) -> p u j t", u=2))
         group_x(scalar_copy, 0)
         quantize_x(0)
         multiply_x(0)

from contextlib import ExitStack

import concourse.mybir as mybir

K, T, S, N = 512, 2048, 768, 256
FLOPS = 2 * 2 * K * N * S

F32 = mybir.dt.float32
BF16 = mybir.dt.bfloat16
I32 = mybir.dt.int32
U32 = mybir.dt.uint32
U16 = mybir.dt.uint16
U8 = mybir.dt.uint8
FP8X4 = mybir.dt.float8_e4m3fn_x4
ACT = mybir.ActivationFunctionType
ALU = mybir.AluOpType

P = 128
PACK = 4
CHUNK = 256
CHUNKS = S // CHUNK
HALVES = N // P
SCALE_WORDS = N // 4

PIECES = ((0, 256), (256, 512), (512, 640), (640, 768))
KIB = 1024
PLANE_AT = (0, 8 * KIB, 32 * KIB, 24 * KIB)


def tile_picked_recall_relu_e_kernel(tc, xT, sT, w1_words, w1_scales, w2_words, w2_scales, b, offs, out):
    nc = tc.nc
    with ExitStack() as ctx:
        keep = ctx.enter_context(tc.tile_pool(name="keep", bufs=1))
        reuse = ctx.enter_context(tc.tile_pool(name="reuse", bufs=1))
        psum = ctx.enter_context(tc.psum_pool(name="psum", bufs=1))

        def placed(shape, dtype, name, offset, align=64):
            return reuse.tile(shape, dtype, name=name, offset=offset, align_bytes=align)

        offsets = keep.tile([P, S // 16], U16, name="offsets")
        s_plane = [placed([P, T], F32, f"s_plane{t}", PLANE_AT[t], 64 if PLANE_AT[t] else 64 * KIB) for t in range(PACK)]
        grouped_at = 40 * KIB
        x_grouped = [placed([P, z - a, PACK], BF16, f"x_grouped{i}", grouped_at + 2 * PACK * a) for i, (a, z) in enumerate(PIECES)]
        w_scale = placed([P, 2, SCALE_WORDS], I32, "w_scale", 70 * KIB)
        bias_rows = placed([P, 32], F32, "bias_rows", 71 * KIB)
        bias = placed([P, 32], F32, "bias", 71 * KIB + 128)
        s_low = placed([P, 2, S], F32, "s_low", 72 * KIB)
        s_high = placed([P, 2, CHUNK], F32, "s_high", 78 * KIB)
        s_outer = placed([P, 4, P, PACK], BF16, "s_outer", 48 * KIB)
        s_middle = placed([P, 2, P, PACK], BF16, "s_middle", 52 * KIB)
        s_grouped = [s_outer[:, 1:3], s_middle[:], s_outer[:, 0:4:3]]
        s_codes = [placed([P, CHUNK], U32, "s_codes0", 64 * KIB)]
        x_codes = placed([P, S], U32, "x_codes", 65 * KIB)
        s_scale = placed([P, S], U8, "s_scale", 46 * KIB)
        x_scale = placed([P, S], U8, "x_scale", 47 * KIB)
        acc = {}
        result = {}

        s_rows = sT.rearrange("(p t) j -> t p j", t=PACK)
        x_rows = xT.rearrange("(p t) j -> p t j", t=PACK)
        out_rows = out.rearrange("(h p) j -> p h j", p=P)

        def cols(c):
            return slice(c * CHUNK, (c + 1) * CHUNK)

        def piece(i):
            return slice(*PIECES[i])

        def width(i):
            return PIECES[i][1] - PIECES[i][0]

        def chunk_of(i):
            return PIECES[i][0] // CHUNK

        def within(i):
            return slice(PIECES[i][0] % CHUNK, PIECES[i][0] % CHUNK + width(i))

        def load_plane(t):
            nc.sync.dma_start(out=s_plane[t][:], in_=s_rows[t])

        def load_scales(queue, w, scales, quadrants):
            rows = scales[0].bitcast(I32)
            for q in quadrants:
                queue.dma_start(out=w_scale[32 * q : 32 * q + 4, w, :], in_=rows[4 * q : 4 * q + 4, :])

        def picked(t, c):
            return s_plane[t][:].indirect(offsets[:, c * (CHUNK // 16) : (c + 1) * (CHUNK // 16)])

        def scalar_copy(dst, src):
            nc.scalar.activation(dst, src, ACT.Copy)

        def quantize_s(c):
            if c < 2:
                nc.vector.quantize_mx(
                    out=s_codes[c][:].bitcast(FP8X4),
                    scales=s_scale[:, cols(c)],
                    in_=s_grouped[c].rearrange("p u j t -> p (u j t)"),
                )
            else:
                for u in range(2):
                    nc.vector.quantize_mx(
                        out=s_codes[c][:, u * P : (u + 1) * P].bitcast(FP8X4),
                        scales=s_scale[:, c * CHUNK + u * P : c * CHUNK + (u + 1) * P],
                        in_=s_grouped[c][:, u].rearrange("p j t -> p (j t)"),
                    )

        def quantize_x(i):
            nc.vector.quantize_mx(
                out=x_codes[:, piece(i)].bitcast(FP8X4),
                scales=x_scale[:, piece(i)],
                in_=x_grouped[i][:].rearrange("p j t -> p (j t)"),
            )

        def relu_scalar(i, h):
            nc.scalar.activation(result[i, h], acc[i, h][:], ACT.Relu, bias=bias[:, h : h + 1])

        def relu_vector(i, h):
            nc.vector.tensor_scalar(result[i, h], acc[i, h][:], bias[:, h : h + 1], 0.0, ALU.add, ALU.max)

        def store_half(i, h):
            nc.sync.dma_start(out=out_rows[:, h, piece(i)], in_=result[i, h])

        def store(i):
            nc.sync.dma_start(out=out_rows[:, :, piece(i)], in_=narrow[i][:])

        nc.vector.memset(w_scale[:], 0)
        nc.vector.memset(bias_rows[:], 0.0)

        load_plane(0)
        nc.sync.dma_start(offsets[:], offs)
        load_plane(1)
        load_plane(2)
        b_rows = b.rearrange("(h q c) o -> h q (c o)", h=HALVES, c=32)
        for h in range(HALVES):
            nc.sync.dma_start(out=bias_rows[h:P:32, :], in_=b_rows[h])
        load_scales(nc.sync, 1, w2_scales, (0, 1, 2))
        load_plane(3)
        load_scales(nc.sync, 1, w2_scales, (3,))
        load_scales(nc.gpsimd, 0, w1_scales, (0, 1, 2, 3))


        nc.vector.tensor_copy(s_low[:, 0, :], s_plane[0][:].indirect(offsets[:]))
        for c in range(CHUNKS):
            nc.vector.tensor_copy(s_low[:, 1, cols(c)], picked(1, c))
            scalar_copy(s_grouped[c][:, :, :, 0:2], s_low[:, :, cols(c)].rearrange("p t (u j) -> p u j t", u=2))
        nc.vector.transpose(bias[:], bias_rows[:])
        for c in (0, 1):
            nc.vector.tensor_copy(s_grouped[c][:, :, :, 2], picked(2, c))
        scalar_copy(s_high[:, 0, :], picked(2, 2))

        x_at = (PLANE_AT[0], None, PLANE_AT[0] + 6144, PLANE_AT[1], PLANE_AT[1] + 2048, PLANE_AT[1] + 4096)
        x_raw = {u: placed([P, PACK, P if u else CHUNK], F32, f"x_raw{u}", x_at[u]) for u in (0, 2, 3, 4, 5)}
        w_both = placed([P, 2 * N], I32, "w_both", PLANE_AT[0] + 4096)
        w_codes = [w_both[:, 0:N], w_both[:, N : 2 * N]]

        def load_x(i):
            nc.sync.dma_start(out=x_raw[i][:], in_=x_rows[:, :, i * P : (i + 1) * P if i else CHUNK])

        def load_codes(w, words):
            nc.sync.dma_start(out=w_codes[w], in_=words[0].rearrange("p m r -> p (m r)").bitcast(I32))

        def group_x(copy, i, part=slice(None)):
            src = x_raw[i][:].rearrange("p t (g e) -> p g t e", e=4)
            home = min(i // 2, 2) + i // 5
            first = i * P - PIECES[home][0]
            dst = x_grouped[home][:, first : first + (P if i else CHUNK), :].rearrange("p (g e) t -> p g t e", e=4)
            copy(dst[:, part], src[:, part])

        def multiply(w, codes, scale, i, first):
            for h in range(HALVES):
                if first:
                    acc[i, h] = psum.tile([P, width(i)], F32, name=f"acc{i}_{h}", tag=f"bank{i}_{h}")
                nc.tensor.matmul_mx(
                    out=acc[i, h][:],
                    lhsT=w_codes[w][:, h * P : (h + 1) * P].bitcast(FP8X4),
                    lhsT_scale=w_scale[:, w, h * P // 4 : (h + 1) * P // 4].bitcast(U8),
                    rhs=codes.bitcast(FP8X4),
                    rhs_scale=scale[:, piece(i)],
                    start=first,
                    stop=not first,
                )

        def multiply_s(i):
            multiply(1, s_codes[chunk_of(i)][:, within(i)], s_scale, i, True)

        def multiply_x(i):
            multiply(0, x_codes[:, piece(i)], x_scale, i, False)

        load_x(0)
        load_codes(1, w2_words)
        load_codes(0, w1_words)
        load_x(2)
        load_x(3)
        load_x(4)
        load_x(5)

        narrow = {i: placed([P, HALVES, P], F32, f"narrow{i}", (66 + i) * KIB) for i in (2, 3)}
        for i in (2, 3):
            for h in range(HALVES):
                result[i, h] = narrow[i][:, h, :]
        for c in (0, 1):
            nc.vector.tensor_copy(s_grouped[c][:, :, :, 3], picked(3, c))
        scalar_copy(s_high[:, 1, :], picked(3, 2))
        quantize_s(0)
        multiply_s(0)
        s_codes.append(placed([P, CHUNK], U32, "s_codes1", PLANE_AT[2]))
        quantize_s(1)
        multiply_s(1)
        nc.vector.tensor_copy(s_grouped[2][:, :, :, 2:4], s_high[:].rearrange("p t (u j) -> p u j t", u=2))
        group_x(scalar_copy, 0)
        quantize_x(0)
        multiply_x(0)
        group_x(scalar_copy, 2)
        group_x(nc.vector.tensor_copy, 3)
        group_x(scalar_copy, 4)
        quantize_x(1)
        multiply_x(1)
        s_codes.append(placed([P, CHUNK], U32, "s_codes2", x_at[2]))
        quantize_s(2)
        multiply_s(2)
        multiply_s(3)
        group_x(nc.vector.tensor_copy, 5)
        quantize_x(2)
        multiply_x(2)
        quantize_x(3)
        multiply_x(3)
        for u, (i, h) in enumerate(((0, 0), (0, 1), (1, 0), (1, 1))):
            result[i, h] = placed([P, CHUNK], F32, f"result{i}_{h}", 48 * KIB + 4 * CHUNK * u)[:]
            relu_scalar(i, h)
            store_half(i, h)
        relu_vector(2, 0)
        relu_vector(2, 1)
        store(2)
        relu_vector(3, 0)
        relu_scalar(3, 1)
        store(3)
